import numpy as np
import ml_dtypes


def mxq(x, axis, fmt="e4m3"):
    dtype, down = {"e4m3": (ml_dtypes.float8_e4m3fn, 7), "e5m2": (ml_dtypes.float8_e5m2, 14)}[fmt]
    v = np.moveaxis(np.asarray(x, np.float32).astype(ml_dtypes.bfloat16).astype(np.float64), axis, -1)
    blocks = v.reshape(v.shape[:-1] + (-1, 32))
    amax = np.abs(blocks).max(-1, keepdims=True)
    byte = np.maximum(np.where(amax > 0, np.frexp(amax)[1] - 1 + 127, 0) - down, 1)
    scale = np.exp2(byte - 127.0)
    codes = (blocks / scale).astype(np.float32).astype(dtype).astype(np.float64)
    return np.moveaxis((codes * scale).reshape(v.shape), -1, axis)


WIDE = False


def mx_kscale(k):
    if not WIDE:
        return np.ones(k)
    levels = np.array([10, -10, 5, -5, 0])
    if k % 512:
        return np.exp2(np.random.permutation(np.resize(levels, k // 32))).repeat(32)
    a = np.empty((k // 512, 16))
    for p in range(k // 512):
        a[p, :8] = np.random.permutation(np.resize(levels, 8))
        for g in range(8):
            far = levels[np.abs(levels - a[p, g]) >= 10]
            a[p, g + 8] = far[np.random.randint(len(far))]
    return np.exp2(a.ravel()).repeat(32)


def f64(x):
    return np.asarray(x).astype(np.float64)


def striped(idx):
    return np.tile(idx.reshape(-1, 16).T, (8, 1)).astype(np.uint16)


def unstriped(offs):
    return offs[:16].T.reshape(-1).astype(np.int64)


def striped8(idx):
    return np.concatenate([x.reshape(-1, 16).T for x in idx]).astype(np.uint16)


def runs(offs, k):
    lists = np.stack([offs[16 * r : 16 * r + 16].T.reshape(-1) for r in range(8)]).astype(np.int64)
    return lists[np.arange(k) % 512 // 64]


def pack_weight(w):
    k, n = w.shape
    w = f64(np.asarray(w, np.float32).astype(ml_dtypes.bfloat16)).reshape(k // 32, 32, n)
    amax = np.abs(w).max(1)
    byte = np.clip(np.where(amax > 0, np.frexp(amax)[1] - 1 + 127 - 7, 1), 1, 254)
    scaled = (w * np.exp2(127.0 - byte)[:, None, :]).reshape(k, n).astype(np.float32)
    words = np.ascontiguousarray(scaled.reshape(k // 512, 128, 4, n).transpose(0, 1, 3, 2)).astype(ml_dtypes.float8_e4m3fn).view(np.uint8)
    return words, np.ascontiguousarray(byte.astype(np.uint8).reshape(k // 512, 16, n))


def unpack_weight(words, scales):
    g, p, n, _ = words.shape
    vals = np.ascontiguousarray(words).view(ml_dtypes.float8_e4m3fn).astype(np.float64) * np.repeat(np.exp2(scales.astype(np.float64) - 127.0), 8, axis=1)[..., None]
    return vals.transpose(0, 1, 3, 2).reshape(g * 512, n)


def sigmoid(v):
    return 1.0 / (1.0 + np.exp(-np.maximum(v, -700.0)))


K, T, S, N, H = 512, 2048, 512, 512, 512


def setup_inputs():
    n = np.random.standard_normal
    s = mx_kscale(K)[:, None]
    u = mx_kscale(H)
    packed_xT = pack_weight(n((K, T)) * s)
    return {
        "x_words": packed_xT[0],
        "x_scales": packed_xT[1],
        "w1": (n((K, H)) / np.sqrt(K) / s).astype(np.float32),
        "gn": (np.random.uniform(0.5, 1.5, (H, 1)) * u[:, None]).astype(np.float32),
        "gm": (np.random.uniform(0.5, 1.5, (H, 1)) * u[:, None]).astype(np.float32),
        "w2": (n((H, N)) / np.sqrt(2 * H) / u[:, None]).astype(np.float32),
        "w3": (n((H, N)) / np.sqrt(2 * H) / u[:, None]).astype(np.float32),
        "offs": striped(np.random.permutation(T)[:S]),
        "n1": striped8(np.stack([np.random.permutation(S) for _ in range(8)])),
        "n2": striped8(np.stack([np.random.permutation(S) for _ in range(8)])),
        "n3": striped8(np.stack([np.random.permutation(S) for _ in range(8)])),
        "n4": striped8(np.stack([np.random.permutation(S) for _ in range(8)])),
        "n5": striped8(np.stack([np.random.permutation(S) for _ in range(8)])),
    }


def reference(x_words, x_scales, w1, gn, gm, w2, w3, offs, n1, n2, n3, n4, n5):
    xq = unpack_weight(x_words, x_scales)[:, unstriped(offs)]
    y = mxq(f64(w1), 0, "e4m3").T @ xq
    ex = np.exp(y)
    z = f64(gn) * (np.log(ex + ex[np.arange(H)[:, None], runs(n1, H)]) - (y[np.arange(H)[:, None], runs(n2, H)]))
    pa = y[np.arange(H)[:, None], runs(n3, H)]
    pb = y[np.arange(H)[:, None], runs(n4, H)]
    z2 = f64(gm) * (np.maximum(np.minimum(y, pa), np.minimum(np.maximum(y, pa), pb)))
    h = mxq(f64(w2), 0, "e4m3").T @ mxq(z, 0, "e4m3") + mxq(f64(w3), 0, "e4m3").T @ mxq(z2, 0, "e4m3")
    return h * (sigmoid(h[np.arange(N)[:, None], runs(n5, N)]))

@@ -1,0 +1,227 @@
+from contextlib import ExitStack
+
+import concourse.mybir as mybir
+
+K, T, S, H, N = 512, 2048, 512, 512, 512
+FLOPS = 2 * K * H * S + 2 * 2 * H * N * S
+
+F32 = mybir.dt.float32
+BF16 = mybir.dt.bfloat16
+I32 = mybir.dt.int32
+U32 = mybir.dt.uint32
+U16 = mybir.dt.uint16
+U8 = mybir.dt.uint8
+FP8X4 = mybir.dt.float8_e4m3fn_x4
+ACT = mybir.ActivationFunctionType
+ALU = mybir.AluOpType
+
+P = 128
+PACK = 4
+HALF = S // 2
+LIST_COLS = S // 16
+HALF_LIST = HALF // 16
+
+
+def tile_picked_joinlsemedgate_none_p_kernel(
+    tc, x_words, x_scales, w1, gn, gm, w2, w3, offs, n1, n2, n3, n4, n5, out
+):
+    nc = tc.nc
+    with ExitStack() as ctx:
+        sb = ctx.enter_context(tc.tile_pool(name="sb", bufs=1))
+        ps = ctx.enter_context(tc.psum_pool(name="ps", bufs=1))
+
+        def load_list(src, name):
+            lst = sb.tile([P, LIST_COLS], U16, name=name)
+            nc.sync.dma_start(lst[:], src)
+            return lst
+
+        def load_weight(src, name):
+            raw = sb.tile([P, PACK, H], F32, name=name)
+            nc.sync.dma_start(raw[:], src.rearrange("(p j) c -> p j c", j=PACK))
+            return raw
+
+        def load_gain(src, name):
+            g = sb.tile([P, PACK], F32, name=name)
+            nc.sync.dma_start(g[:], src.rearrange("(p t) o -> p (t o)", t=PACK))
+            return g
+
+        def half_cols(hf):
+            return slice(hf * HALF, (hf + 1) * HALF)
+
+        def half_list(lst, hf):
+            return lst[:, hf * HALF_LIST : (hf + 1) * HALF_LIST]
+
+        def dealt_views(raw, dealt, m0, m1):
+            src = raw[:].rearrange("p j (m t) -> p m t j", t=PACK)[:, m0:m1]
+            dst = dealt[:].rearrange("p (t m j) -> p m t j", t=PACK, j=PACK)[:, m0:m1]
+            return dst, src
+
+        def quantize(values, width, name):
+            codes = sb.tile([P, width], U32, name=name + "_codes", align_bytes=64)
+            scales = sb.tile([P, width], U8, name=name + "_scales", align_bytes=64)
+            nc.vector.quantize_mx(out=codes[:].bitcast(FP8X4), scales=scales[:], in_=values)
+            return codes, scales
+
+        def interleave(copy, planes, width, name):
+            woven = sb.tile([P, width * PACK], BF16, name=name, align_bytes=64)
+            copy(
+                out=woven[:].rearrange("p (c i t) -> p c t i", i=PACK, t=PACK),
+                in_=planes[:].rearrange("p t (c i) -> p c t i", i=PACK),
+            )
+            return woven
+
+        def pool_cast(dst, src):
+            nc.gpsimd.tensor_scalar(out=dst, in0=src, scalar1=1.0, scalar2=0.0, op0=ALU.mult, op1=ALU.add)
+
+        def product(acc, wq, t, xq, cols, start, stop):
+            m_cols = slice(t * P, (t + 1) * P)
+            nc.tensor.matmul_mx(
+                out=acc,
+                lhsT=wq[0][:, m_cols].bitcast(FP8X4),
+                lhsT_scale=wq[1][:, m_cols],
+                rhs=xq[0][:, cols].bitcast(FP8X4),
+                rhs_scale=xq[1][:, cols],
+                start=start,
+                stop=stop,
+            )
+
+        scale_table = sb.tile([P, T], U8, name="scale_table")
+        nc.vector.memset(scale_table[:].bitcast(I32), 0)
+        offs_l = load_list(offs, "offs_l")
+        w1_raw = load_weight(w1, "w1_raw")
+        for r in range(PACK):
+            nc.sync.dma_start(scale_table[r:P:32, :].bitcast(I32), x_scales[0, r:16:PACK, :].bitcast(I32))
+        word_table = sb.tile([P, T], U32, name="word_table")
+        nc.sync.dma_start(word_table[:].bitcast(I32), x_words[0].rearrange("p c r -> p (c r)").bitcast(I32))
+        gm_t = load_gain(gm, "gm_t")
+        n3_l = load_list(n3, "n3_l")
+        n4_l = load_list(n4, "n4_l")
+        n1_l = load_list(n1, "n1_l")
+        gn_t = load_gain(gn, "gn_t")
+        n2_l = load_list(n2, "n2_l")
+        n5_l = load_list(n5, "n5_l")
+        w3_raw = load_weight(w3, "w3_raw")
+        w2_raw = load_weight(w2, "w2_raw")
+
+        w1_dealt = sb.tile([P, H * PACK], BF16, name="w1_dealt", align_bytes=64)
+        dst, src = dealt_views(w1_raw, w1_dealt, 0, 48)
+        nc.scalar.activation(dst, src, ACT.Copy)
+        dst, src = dealt_views(w1_raw, w1_dealt, 48, P)
+        nc.vector.tensor_copy(out=dst, in_=src)
+        x_sc = sb.tile([P, S], U8, name="x_sc", align_bytes=64)
+        nc.vector.tensor_copy(out=x_sc[:], in_=scale_table[:].indirect(offs_l[:]))
+        w1q = quantize(w1_dealt[:], H, "w1q")
+        x_wd = sb.tile([P, S], U32, name="x_wd", align_bytes=64)
+        nc.vector.tensor_copy(out=x_wd[:], in_=word_table[:].indirect(offs_l[:]))
+        xq = (x_wd, x_sc)
+
+        y_ps = []
+        for t in range(PACK):
+            acc = ps.tile([P, S], F32, name="y_ps%d" % t, tag="bank%d" % t)
+            product(acc[:], w1q, t, xq, slice(0, S), True, True)
+            y_ps.append(acc)
+
+        gmy = [sb.tile([P, 2 * S], F32, name="gmy%d" % t) for t in range(PACK)]
+        y = [sb.tile([P, 2 * S], F32, name="y%d" % t) for t in range(PACK)]
+        ex1 = sb.tile([P, PACK, S], F32, name="ex1")
+        exsum = sb.tile([P, PACK, S], F32, name="exsum")
+        lse = sb.tile([P, PACK, S], F32, name="lse")
+        yb = sb.tile([P, PACK, S], BF16, name="yb")
+        pa = sb.tile([P, PACK, S], BF16, name="pa")
+        pb = sb.tile([P, PACK, S], BF16, name="pb")
+        lo = sb.tile([P, PACK, S], BF16, name="lo")
+        hi = sb.tile([P, PACK, S], BF16, name="hi")
+        above = sb.tile([P, PACK, S], BF16, name="above")
+        med = sb.tile([P, PACK, S], BF16, name="med")
+
+        def scaled_y(t):
+            nc.scalar.activation(gmy[t][:, :S], y_ps[t][:], ACT.Copy, scale=gm_t[:, t : t + 1])
+
+        def exps(t):
+            nc.scalar.activation(y[t][:, :S], y_ps[t][:], ACT.Copy)
+            nc.scalar.activation(y[t][:, S:], y_ps[t][:], ACT.Exp)
+            nc.scalar.activation(ex1[:, t, :], y[t][:].indirect(n1_l[:]), ACT.Exp)
+
+        def neighbours(t):
+            for dst_tile, lst in ((pa, n3_l), (pb, n4_l)):
+                nc.vector.tensor_copy(out=dst_tile[:, t, :], in_=gmy[t][:].indirect(lst[:]))
+
+        def add_exps(t):
+            nc.vector.tensor_tensor(out=exsum[:, t, :], in0=y[t][:, S:], in1=ex1[:, t, :], op=ALU.add)
+
+        neg_gn = sb.tile([P, PACK], F32, name="neg_gn")
+        nc.scalar.activation(neg_gn[:], gn_t[:], ACT.Copy, scale=-1.0)
+        w3_dealt = sb.tile([P, N * PACK], BF16, name="w3_dealt", align_bytes=64)
+        pool_cast(*dealt_views(w3_raw, w3_dealt, 0, P))
+        w2_dealt = sb.tile([P, N * PACK], BF16, name="w2_dealt", align_bytes=64)
+        pool_cast(*dealt_views(w2_raw, w2_dealt, 0, P))
+
+        scaled_y(0)
+        for t in range(PACK):
+            if t + 1 < PACK:
+                scaled_y(t + 1)
+            exps(t)
+            neighbours(t)
+            pool_cast(yb[:, t, :], gmy[t][:, :S])
+        for t in range(PACK - 1):
+            add_exps(t)
+        nc.vector.tensor_tensor(out=lo[:], in0=pa[:], in1=pb[:], op=ALU.min)
+        add_exps(PACK - 1)
+        nc.vector.tensor_tensor(out=hi[:], in0=pa[:], in1=pb[:], op=ALU.max)
+        for t in range(PACK):
+            nc.scalar.activation(lse[:, t, :], exsum[:, t, :], ACT.Ln)
+        warm = sb.tile([P, 1], F32, name="warm")
+        nc.scalar.activation(warm[:], lse[:, PACK - 1, 0:1], ACT.Sigmoid)
+        nc.vector.tensor_tensor(out=above[:], in0=yb[:], in1=lo[:], op=ALU.max)
+        nc.vector.tensor_tensor(out=med[:], in0=above[:], in1=hi[:], op=ALU.min)
+        z2_woven = interleave(nc.scalar.copy, med, S, "z2_woven")
+
+        diff = [sb.tile([P, PACK, HALF], F32, name="diff%d" % hf) for hf in range(2)]
+        zb = [sb.tile([P, PACK, HALF], BF16, name="zb%d" % hf) for hf in range(2)]
+
+        def subtract(hf, t):
+            nc.vector.tensor_tensor(
+                out=diff[hf][:, t, :], in0=y[t][:].indirect(half_list(n2_l, hf)), in1=lse[:, t, half_cols(hf)], op=ALU.subtract
+            )
+            nc.scalar.activation(zb[hf][:, t, :], diff[hf][:, t, :], ACT.Copy, scale=neg_gn[:, t : t + 1])
+
+        for t in range(PACK):
+            subtract(0, t)
+        z_woven0 = interleave(nc.scalar.copy, zb[0], HALF, "z_woven0")
+        w3q = quantize(w3_dealt[:], N, "w3q")
+        w2q = quantize(w2_dealt[:], N, "w2q")
+        z2q = quantize(z2_woven[:], S, "z2q")
+        for t in range(PACK):
+            subtract(1, t)
+        zq0 = quantize(z_woven0[:], HALF, "zq0")
+        z_woven1 = interleave(nc.vector.tensor_copy, zb[1], HALF, "z_woven1")
+        zq1 = quantize(z_woven1[:], HALF, "zq1")
+        zq = [zq0, zq1]
+
+        h = [sb.tile([P, S], F32, name="h%d" % t) for t in range(PACK)]
+        sig = [sb.tile([P, S], F32, name="sig%d" % t) for t in range(PACK)]
+        for hf in range(2):
+            for t in range(PACK):
+                acc = ps.tile([P, HALF], F32, name="h_ps%d_%d" % (hf, t), tag="bank%d" % (t + PACK * (1 - hf)))
+                product(acc[:], w3q, t, z2q, half_cols(hf), True, False)
+                product(acc[:], w2q, t, zq[hf], slice(0, HALF), False, True)
+                if t < 2:
+                    nc.scalar.activation(sig[t][:, half_cols(hf)], acc[:], ACT.Sigmoid)
+                if t < 2 and hf == 1:
+                    nc.vector.tensor_copy(out=h[t][:, half_cols(hf)], in_=acc[:])
+                else:
+                    nc.scalar.activation(h[t][:, half_cols(hf)], acc[:], ACT.Copy)
+
+        out_rows = out.rearrange("(p t) n -> t p n", t=PACK)
+        res = [sb.tile([P, S], F32, name="res%d" % t) for t in range(PACK)]
+        for t in range(2):
+            for hf in range(2):
+                nc.vector.tensor_tensor(
+                    out=res[t][:, half_cols(hf)], in0=sig[t][:].indirect(half_list(n5_l, hf)), in1=h[t][:, half_cols(hf)], op=ALU.mult
+                )
+            nc.sync.dma_start(out_rows[t], res[t][:])
+        for t in range(2, PACK):
+            for hf in range(2):
+                nc.scalar.activation(sig[t][:, half_cols(hf)], h[t][:].indirect(half_list(n5_l, hf)), ACT.Sigmoid)
+            nc.vector.tensor_tensor(out=res[t][:], in0=sig[t][:], in1=h[t][:], op=ALU.mult)
+            nc.sync.dma_start(out_rows[t], res[t][:])

@@ -57,7 +57,7 @@ def tile_picked_joinlsemedgate_none_p_kernel(
             return dst, src
 
         def quantize(values, width, name):
-            codes = sb.tile([P, width], U32, name=name + "_codes", align_bytes=64)
+            codes = sb.tile([P, width], U32, name=name + "_codes", tag=name + "_codes", align_bytes=64)
             scales = sb.tile([P, width], U8, name=name + "_scales", align_bytes=64)
             nc.vector.quantize_mx(out=codes[:].bitcast(FP8X4), scales=scales[:], in_=values)
             return codes, scales
@@ -66,12 +66,9 @@ def tile_picked_joinlsemedgate_none_p_kernel(
             woven = sb.tile([P, width * PACK], BF16, name=name, align_bytes=64)
             copy(
                 out=woven[:].rearrange("p (c i t) -> p c t i", i=PACK, t=PACK),
-                in_=planes[:].rearrange("p t (c i) -> p c t i", i=PACK),
+                in_=planes.rearrange("p t (c i) -> p c t i", i=PACK),
             )
             return woven
-
-        def pool_cast(dst, src):
-            nc.gpsimd.tensor_scalar(out=dst, in0=src, scalar1=1.0, scalar2=0.0, op0=ALU.mult, op1=ALU.add)
 
         def product(acc, wq, t, xq, cols, start, stop):
             m_cols = slice(t * P, (t + 1) * P)
@@ -104,22 +101,26 @@ def tile_picked_joinlsemedgate_none_p_kernel(
         w2_raw = load_weight(w2, "w2_raw")
 
         w1_dealt = sb.tile([P, H * PACK], BF16, name="w1_dealt", align_bytes=64)
-        dst, src = dealt_views(w1_raw, w1_dealt, 0, 48)
+        dst, src = dealt_views(w1_raw, w1_dealt, 0, 64)
         nc.scalar.activation(dst, src, ACT.Copy)
-        dst, src = dealt_views(w1_raw, w1_dealt, 48, P)
+        dst, src = dealt_views(w1_raw, w1_dealt, 64, P)
         nc.vector.tensor_copy(out=dst, in_=src)
         x_sc = sb.tile([P, S], U8, name="x_sc", align_bytes=64)
         nc.vector.tensor_copy(out=x_sc[:], in_=scale_table[:].indirect(offs_l[:]))
         w1q = quantize(w1_dealt[:], H, "w1q")
         x_wd = sb.tile([P, S], U32, name="x_wd", align_bytes=64)
-        nc.vector.tensor_copy(out=x_wd[:], in_=word_table[:].indirect(offs_l[:]))
+        for hf in range(2):
+            nc.vector.tensor_copy(out=x_wd[:, half_cols(hf)], in_=word_table[:].indirect(half_list(offs_l, hf)))
         xq = (x_wd, x_sc)
 
         y_ps = []
         for t in range(PACK):
-            acc = ps.tile([P, S], F32, name="y_ps%d" % t, tag="bank%d" % t)
-            product(acc[:], w1q, t, xq, slice(0, S), True, True)
-            y_ps.append(acc)
+            pieces = []
+            for k, cols in enumerate([half_cols(0), half_cols(1)] if t == 0 else [slice(0, S)]):
+                acc = ps.tile([P, cols.stop - cols.start], F32, name="y_ps%d_%d" % (t, k), tag="bank%d" % (t + PACK * k))
+                product(acc[:], w1q, t, xq, cols, True, True)
+                pieces.append((cols, acc))
+            y_ps.append(pieces)
 
         gmy = [sb.tile([P, 2 * S], F32, name="gmy%d" % t) for t in range(PACK)]
         y = [sb.tile([P, 2 * S], F32, name="y%d" % t) for t in range(PACK)]
@@ -135,11 +136,16 @@ def tile_picked_joinlsemedgate_none_p_kernel(
         med = sb.tile([P, PACK, S], BF16, name="med")
 
         def scaled_y(t):
-            nc.scalar.activation(gmy[t][:, :S], y_ps[t][:], ACT.Copy, scale=gm_t[:, t : t + 1])
+            for k, (cols, acc) in enumerate(y_ps[t]):
+                if k == 0 and t == 0:
+                    nc.vector.tensor_scalar(out=gmy[t][:, cols], in0=acc[:], scalar1=gm_t[:, t : t + 1], scalar2=None, op0=ALU.mult)
+                else:
+                    nc.scalar.activation(gmy[t][:, cols], acc[:], ACT.Copy, scale=gm_t[:, t : t + 1])
 
         def exps(t):
-            nc.scalar.activation(y[t][:, :S], y_ps[t][:], ACT.Copy)
-            nc.scalar.activation(y[t][:, S:], y_ps[t][:], ACT.Exp)
+            for cols, acc in y_ps[t]:
+                nc.scalar.activation(y[t][:, cols], acc[:], ACT.Copy)
+                nc.scalar.activation(y[t][:, S + cols.start : S + cols.stop], acc[:], ACT.Exp)
             nc.scalar.activation(ex1[:, t, :], y[t][:].indirect(n1_l[:]), ACT.Exp)
 
         def neighbours(t):
@@ -150,31 +156,31 @@ def tile_picked_joinlsemedgate_none_p_kernel(
             nc.vector.tensor_tensor(out=exsum[:, t, :], in0=y[t][:, S:], in1=ex1[:, t, :], op=ALU.add)
 
         neg_gn = sb.tile([P, PACK], F32, name="neg_gn")
-        nc.scalar.activation(neg_gn[:], gn_t[:], ACT.Copy, scale=-1.0)
-        w3_dealt = sb.tile([P, N * PACK], BF16, name="w3_dealt", align_bytes=64)
-        pool_cast(*dealt_views(w3_raw, w3_dealt, 0, P))
-        w2_dealt = sb.tile([P, N * PACK], BF16, name="w2_dealt", align_bytes=64)
-        pool_cast(*dealt_views(w2_raw, w2_dealt, 0, P))
-
+        nc.vector.tensor_scalar(out=neg_gn[:], in0=gn_t[:], scalar1=-1.0, scalar2=None, op0=ALU.mult)
         scaled_y(0)
         for t in range(PACK):
             if t + 1 < PACK:
                 scaled_y(t + 1)
             exps(t)
             neighbours(t)
-            pool_cast(yb[:, t, :], gmy[t][:, :S])
+        for t in range(PACK):
+            for cols, acc in y_ps[t]:
+                nc.scalar.activation(yb[:, t, cols], acc[:], ACT.Copy, scale=gm_t[:, t : t + 1])
         for t in range(PACK - 1):
             add_exps(t)
         nc.vector.tensor_tensor(out=lo[:], in0=pa[:], in1=pb[:], op=ALU.min)
         add_exps(PACK - 1)
         nc.vector.tensor_tensor(out=hi[:], in0=pa[:], in1=pb[:], op=ALU.max)
-        for t in range(PACK):
-            nc.scalar.activation(lse[:, t, :], exsum[:, t, :], ACT.Ln)
-        warm = sb.tile([P, 1], F32, name="warm")
-        nc.scalar.activation(warm[:], lse[:, PACK - 1, 0:1], ACT.Sigmoid)
-        nc.vector.tensor_tensor(out=above[:], in0=yb[:], in1=lo[:], op=ALU.max)
-        nc.vector.tensor_tensor(out=med[:], in0=above[:], in1=hi[:], op=ALU.min)
-        z2_woven = interleave(nc.scalar.copy, med, S, "z2_woven")
+        for hf in range(2):
+            nc.scalar.activation(lse[:, :, half_cols(hf)], exsum[:, :, half_cols(hf)], ACT.Ln)
+        w3_dealt = sb.tile([P, N * PACK], BF16, name="w3_dealt", tag="w1q_codes", align_bytes=64)
+        nc.scalar.activation(*dealt_views(w3_raw, w3_dealt, 0, P), ACT.Copy)
+        for hf in range(2):
+            nc.vector.tensor_tensor(out=above[:, :, half_cols(hf)], in0=yb[:, :, half_cols(hf)], in1=lo[:, :, half_cols(hf)], op=ALU.max)
+        for hf in range(2):
+            nc.vector.tensor_tensor(out=med[:, :, half_cols(hf)], in0=above[:, :, half_cols(hf)], in1=hi[:, :, half_cols(hf)], op=ALU.min)
+        z2_woven = [interleave(nc.vector.tensor_copy, med[:, :, half_cols(hf)], HALF, "z2_woven%d" % hf) for hf in range(2)]
+        z2q = [quantize(z2_woven[hf][:], HALF, "z2q%d" % hf) for hf in range(2)]
 
         diff = [sb.tile([P, PACK, HALF], F32, name="diff%d" % hf) for hf in range(2)]
         zb = [sb.tile([P, PACK, HALF], BF16, name="zb%d" % hf) for hf in range(2)]
@@ -183,27 +189,41 @@ def tile_picked_joinlsemedgate_none_p_kernel(
             nc.vector.tensor_tensor(
                 out=diff[hf][:, t, :], in0=y[t][:].indirect(half_list(n2_l, hf)), in1=lse[:, t, half_cols(hf)], op=ALU.subtract
             )
-            nc.scalar.activation(zb[hf][:, t, :], diff[hf][:, t, :], ACT.Copy, scale=neg_gn[:, t : t + 1])
+
+        def gain(hf, t):
+            nc.vector.tensor_scalar(
+                out=zb[hf][:, t, :], in0=diff[hf][:, t, :], scalar1=gn_t[:, t : t + 1], scalar2=-1.0, op0=ALU.mult, op1=ALU.mult
+            )
 
         for t in range(PACK):
             subtract(0, t)
-        z_woven0 = interleave(nc.scalar.copy, zb[0], HALF, "z_woven0")
+            nc.scalar.activation(zb[0][:, t, :], diff[0][:, t, :], ACT.Copy, scale=neg_gn[:, t : t + 1])
+        w2_dealt = sb.tile([P, N * PACK], BF16, name="w2_dealt", align_bytes=64)
+        nc.scalar.activation(*dealt_views(w2_raw, w2_dealt, 0, P), ACT.Copy)
+        warm = sb.tile([P, 1], F32, name="warm")
+        nc.scalar.activation(warm[:], lse[:, PACK - 1, S - 1 : S], ACT.Sigmoid)
         w3q = quantize(w3_dealt[:], N, "w3q")
-        w2q = quantize(w2_dealt[:], N, "w2q")
-        z2q = quantize(z2_woven[:], S, "z2q")
-        for t in range(PACK):
-            subtract(1, t)
+        subtract(1, 0)
+        z_woven0 = interleave(nc.vector.tensor_copy, zb[0][:], HALF, "z_woven0")
+        subtract(1, 1)
         zq0 = quantize(z_woven0[:], HALF, "zq0")
-        z_woven1 = interleave(nc.vector.tensor_copy, zb[1], HALF, "z_woven1")
+        w2q = quantize(w2_dealt[:], N, "w2q")
+        subtract(1, 2)
+        gain(1, 0)
+        subtract(1, 3)
+        gain(1, 1)
+        gain(1, 2)
+        gain(1, 3)
+        z_woven1 = interleave(nc.vector.tensor_copy, zb[1][:], HALF, "z_woven1")
         zq1 = quantize(z_woven1[:], HALF, "zq1")
         zq = [zq0, zq1]
 
-        h = [sb.tile([P, S], F32, name="h%d" % t) for t in range(PACK)]
-        sig = [sb.tile([P, S], F32, name="sig%d" % t) for t in range(PACK)]
+        h = [sb.tile([P, 2 * S], F32, name="h%d" % t) for t in range(PACK)]
+        sig = [sb.tile([P, 2 * S], F32, name="sig%d" % t) for t in range(PACK)]
         for hf in range(2):
             for t in range(PACK):
-                acc = ps.tile([P, HALF], F32, name="h_ps%d_%d" % (hf, t), tag="bank%d" % (t + PACK * (1 - hf)))
-                product(acc[:], w3q, t, z2q, half_cols(hf), True, False)
+                acc = ps.tile([P, HALF], F32, name="h_ps%d_%d" % (hf, t), tag="bank%d" % ((t + 1) % PACK + PACK if hf == 0 else t))
+                product(acc[:], w3q, t, z2q[hf], slice(0, HALF), True, False)
                 product(acc[:], w2q, t, zq[hf], slice(0, HALF), False, True)
                 if t < 2:
                     nc.scalar.activation(sig[t][:, half_cols(hf)], acc[:], ACT.Sigmoid)
@@ -215,13 +235,13 @@ def tile_picked_joinlsemedgate_none_p_kernel(
         out_rows = out.rearrange("(p t) n -> t p n", t=PACK)
         res = [sb.tile([P, S], F32, name="res%d" % t) for t in range(PACK)]
         for t in range(2):
-            for hf in range(2):
-                nc.vector.tensor_tensor(
-                    out=res[t][:, half_cols(hf)], in0=sig[t][:].indirect(half_list(n5_l, hf)), in1=h[t][:, half_cols(hf)], op=ALU.mult
-                )
+            nc.vector.tensor_tensor(out=res[t][:], in0=sig[t][:].indirect(n5_l[:]), in1=h[t][:, :S], op=ALU.mult)
             nc.sync.dma_start(out_rows[t], res[t][:])
-        for t in range(2, PACK):
-            for hf in range(2):
-                nc.scalar.activation(sig[t][:, half_cols(hf)], h[t][:].indirect(half_list(n5_l, hf)), ACT.Sigmoid)
-            nc.vector.tensor_tensor(out=res[t][:], in0=sig[t][:], in1=h[t][:], op=ALU.mult)
-            nc.sync.dma_start(out_rows[t], res[t][:])
+        nc.scalar.activation(sig[2][:, :S], h[2][:].indirect(n5_l[:]), ACT.Sigmoid)
+        nc.vector.tensor_tensor(out=res[2][:], in0=sig[2][:, :S], in1=h[2][:, :S], op=ALU.mult)
+        nc.sync.dma_start(out_rows[2], res[2][:])
+        for hf in range(2):
+            cols = half_cols(hf)
+            nc.scalar.activation(sig[3][:, cols], h[3][:].indirect(half_list(n5_l, hf)), ACT.Sigmoid)
+            nc.vector.tensor_tensor(out=res[3][:, cols], in0=sig[3][:, cols], in1=h[3][:, cols], op=ALU.mult)
+            nc.sync.dma_start(out_rows[3][:, cols], res[3][:, cols])

@@ -18,8 +18,9 @@ ALU = mybir.AluOpType
 P = 128
 PACK = 4
 HALF = S // 2
-LIST_COLS = S // 16
-HALF_LIST = HALF // 16
+HALVES = (slice(0, HALF), slice(HALF, S))
+W1_SCALAR_COLS = 64
+FUSED_PLANES = 2
 
 
 def tile_picked_joinlsemedgate_none_p_kernel(
@@ -31,7 +32,7 @@ def tile_picked_joinlsemedgate_none_p_kernel(
         ps = ctx.enter_context(tc.psum_pool(name="ps", bufs=1))
 
         def load_list(src, name):
-            lst = sb.tile([P, LIST_COLS], U16, name=name)
+            lst = sb.tile([P, S // 16], U16, name=name)
             nc.sync.dma_start(lst[:], src)
             return lst
 
@@ -41,15 +42,12 @@ def tile_picked_joinlsemedgate_none_p_kernel(
             return raw
 
         def load_gain(src, name):
-            g = sb.tile([P, PACK], F32, name=name)
-            nc.sync.dma_start(g[:], src.rearrange("(p t) o -> p (t o)", t=PACK))
-            return g
+            gain = sb.tile([P, PACK], F32, name=name)
+            nc.sync.dma_start(gain[:], src.rearrange("(p t) o -> p (t o)", t=PACK))
+            return gain
 
-        def half_cols(hf):
-            return slice(hf * HALF, (hf + 1) * HALF)
-
-        def half_list(lst, hf):
-            return lst[:, hf * HALF_LIST : (hf + 1) * HALF_LIST]
+        def entries(lst, cols):
+            return lst[:, cols.start // 16 : cols.stop // 16]
 
         def dealt_views(raw, dealt, m0, m1):
             src = raw[:].rearrange("p j (m t) -> p m t j", t=PACK)[:, m0:m1]
@@ -58,13 +56,13 @@ def tile_picked_joinlsemedgate_none_p_kernel(
 
         def quantize(values, width, name):
             codes = sb.tile([P, width], U32, name=name + "_codes", tag=name + "_codes", align_bytes=64)
-            scales = sb.tile([P, width], U8, name=name + "_scales", align_bytes=64)
+            scales = sb.tile([P, width], U8, name=name + "_scales", tag=name + "_scales", align_bytes=64)
             nc.vector.quantize_mx(out=codes[:].bitcast(FP8X4), scales=scales[:], in_=values)
             return codes, scales
 
-        def interleave(copy, planes, width, name):
-            woven = sb.tile([P, width * PACK], BF16, name=name, align_bytes=64)
-            copy(
+        def weave(planes, name):
+            woven = sb.tile([P, HALF * PACK], BF16, name=name, tag=name, align_bytes=64)
+            nc.vector.tensor_copy(
                 out=woven[:].rearrange("p (c i t) -> p c t i", i=PACK, t=PACK),
                 in_=planes.rearrange("p t (c i) -> p c t i", i=PACK),
             )
@@ -73,7 +71,7 @@ def tile_picked_joinlsemedgate_none_p_kernel(
         def product(acc, wq, t, xq, cols, start, stop):
             m_cols = slice(t * P, (t + 1) * P)
             nc.tensor.matmul_mx(
-                out=acc,
+                out=acc[:],
                 lhsT=wq[0][:, m_cols].bitcast(FP8X4),
                 lhsT_scale=wq[1][:, m_cols],
                 rhs=xq[0][:, cols].bitcast(FP8X4),
@@ -101,147 +99,130 @@ def tile_picked_joinlsemedgate_none_p_kernel(
         w2_raw = load_weight(w2, "w2_raw")
 
         w1_dealt = sb.tile([P, H * PACK], BF16, name="w1_dealt", align_bytes=64)
-        dst, src = dealt_views(w1_raw, w1_dealt, 0, 64)
-        nc.scalar.activation(dst, src, ACT.Copy)
-        dst, src = dealt_views(w1_raw, w1_dealt, 64, P)
-        nc.vector.tensor_copy(out=dst, in_=src)
-        x_sc = sb.tile([P, S], U8, name="x_sc", align_bytes=64)
-        nc.vector.tensor_copy(out=x_sc[:], in_=scale_table[:].indirect(offs_l[:]))
+        nc.scalar.activation(*dealt_views(w1_raw, w1_dealt, 0, W1_SCALAR_COLS), ACT.Copy)
+        nc.vector.tensor_copy(*dealt_views(w1_raw, w1_dealt, W1_SCALAR_COLS, P))
+        x_picked_scales = sb.tile([P, S], U8, name="x_picked_scales", align_bytes=64)
+        nc.vector.tensor_copy(out=x_picked_scales[:], in_=scale_table[:].indirect(offs_l[:]))
         w1q = quantize(w1_dealt[:], H, "w1q")
-        x_wd = sb.tile([P, S], U32, name="x_wd", align_bytes=64)
-        for hf in range(2):
-            nc.vector.tensor_copy(out=x_wd[:, half_cols(hf)], in_=word_table[:].indirect(half_list(offs_l, hf)))
-        xq = (x_wd, x_sc)
+        x_picked_words = sb.tile([P, S], U32, name="x_picked_words", align_bytes=64)
+        for cols in HALVES:
+            nc.vector.tensor_copy(out=x_picked_words[:, cols], in_=word_table[:].indirect(entries(offs_l, cols)))
+        xq = (x_picked_words, x_picked_scales)
+        neg_gn = sb.tile([P, PACK], F32, name="neg_gn")
+        nc.scalar.activation(neg_gn[:], gn_t[:], ACT.Copy, scale=-1.0)
 
         y_ps = []
         for t in range(PACK):
             pieces = []
-            for k, cols in enumerate([half_cols(0), half_cols(1)] if t == 0 else [slice(0, S)]):
+            for k, cols in enumerate(HALVES if t == 0 else (slice(0, S),)):
                 acc = ps.tile([P, cols.stop - cols.start], F32, name="y_ps%d_%d" % (t, k), tag="bank%d" % (t + PACK * k))
-                product(acc[:], w1q, t, xq, cols, True, True)
+                product(acc, w1q, t, xq, cols, True, True)
                 pieces.append((cols, acc))
             y_ps.append(pieces)
 
-        gmy = [sb.tile([P, 2 * S], F32, name="gmy%d" % t) for t in range(PACK)]
-        y = [sb.tile([P, 2 * S], F32, name="y%d" % t) for t in range(PACK)]
-        ex1 = sb.tile([P, PACK, S], F32, name="ex1")
-        exsum = sb.tile([P, PACK, S], F32, name="exsum")
-        lse = sb.tile([P, PACK, S], F32, name="lse")
-        yb = sb.tile([P, PACK, S], BF16, name="yb")
+        gm_y = [sb.tile([P, 2 * S], F32, name="gm_y%d" % t) for t in range(PACK)]
+        y_ex = [sb.tile([P, 2 * S], F32, name="y_ex%d" % t) for t in range(PACK)]
+        ex_n1 = sb.tile([P, PACK, S], F32, name="ex_n1")
+        ex_sum = sb.tile([P, PACK, S], F32, name="ex_sum")
+        log_sum = sb.tile([P, PACK, S], F32, name="log_sum")
+        own = sb.tile([P, PACK, S], BF16, name="own")
         pa = sb.tile([P, PACK, S], BF16, name="pa")
         pb = sb.tile([P, PACK, S], BF16, name="pb")
-        lo = sb.tile([P, PACK, S], BF16, name="lo")
-        hi = sb.tile([P, PACK, S], BF16, name="hi")
+        low = sb.tile([P, PACK, S], BF16, name="low")
+        high = sb.tile([P, PACK, S], BF16, name="high")
         above = sb.tile([P, PACK, S], BF16, name="above")
-        med = sb.tile([P, PACK, S], BF16, name="med")
+        z2 = sb.tile([P, PACK, S], BF16, name="z2")
 
-        def scaled_y(t):
-            for k, (cols, acc) in enumerate(y_ps[t]):
-                if k == 0 and t == 0:
-                    nc.vector.tensor_scalar(out=gmy[t][:, cols], in0=acc[:], scalar1=gm_t[:, t : t + 1], scalar2=None, op0=ALU.mult)
-                else:
-                    nc.scalar.activation(gmy[t][:, cols], acc[:], ACT.Copy, scale=gm_t[:, t : t + 1])
-
-        def exps(t):
-            for cols, acc in y_ps[t]:
-                nc.scalar.activation(y[t][:, cols], acc[:], ACT.Copy)
-                nc.scalar.activation(y[t][:, S + cols.start : S + cols.stop], acc[:], ACT.Exp)
-            nc.scalar.activation(ex1[:, t, :], y[t][:].indirect(n1_l[:]), ACT.Exp)
-
-        def neighbours(t):
-            for dst_tile, lst in ((pa, n3_l), (pb, n4_l)):
-                nc.vector.tensor_copy(out=dst_tile[:, t, :], in_=gmy[t][:].indirect(lst[:]))
+        def scale_y(dst, t, acc):
+            nc.scalar.activation(dst, acc[:], ACT.Copy, scale=gm_t[:, t : t + 1])
 
         def add_exps(t):
-            nc.vector.tensor_tensor(out=exsum[:, t, :], in0=y[t][:, S:], in1=ex1[:, t, :], op=ALU.add)
+            nc.vector.tensor_tensor(out=ex_sum[:, t, :], in0=y_ex[t][:, S:], in1=ex_n1[:, t, :], op=ALU.add)
 
-        neg_gn = sb.tile([P, PACK], F32, name="neg_gn")
-        nc.vector.tensor_scalar(out=neg_gn[:], in0=gn_t[:], scalar1=-1.0, scalar2=None, op0=ALU.mult)
-        scaled_y(0)
+        (first_cols, first_acc), (second_cols, second_acc) = y_ps[0]
+        nc.vector.tensor_scalar(out=gm_y[0][:, first_cols], in0=first_acc[:], scalar1=gm_t[:, 0:1], scalar2=None, op0=ALU.mult)
+        scale_y(gm_y[0][:, second_cols], 0, second_acc)
         for t in range(PACK):
             if t + 1 < PACK:
-                scaled_y(t + 1)
-            exps(t)
-            neighbours(t)
+                for cols, acc in y_ps[t + 1]:
+                    scale_y(gm_y[t + 1][:, cols], t + 1, acc)
+            for cols, acc in y_ps[t]:
+                nc.scalar.activation(y_ex[t][:, cols], acc[:], ACT.Copy)
+                nc.scalar.activation(y_ex[t][:, S + cols.start : S + cols.stop], acc[:], ACT.Exp)
+            nc.scalar.activation(ex_n1[:, t, :], y_ex[t][:].indirect(n1_l[:]), ACT.Exp)
+            nc.vector.tensor_copy(out=pa[:, t, :], in_=gm_y[t][:].indirect(n3_l[:]))
+            nc.vector.tensor_copy(out=pb[:, t, :], in_=gm_y[t][:].indirect(n4_l[:]))
         for t in range(PACK):
             for cols, acc in y_ps[t]:
-                nc.scalar.activation(yb[:, t, cols], acc[:], ACT.Copy, scale=gm_t[:, t : t + 1])
+                scale_y(own[:, t, cols], t, acc)
+
         for t in range(PACK - 1):
             add_exps(t)
-        nc.vector.tensor_tensor(out=lo[:], in0=pa[:], in1=pb[:], op=ALU.min)
+        nc.vector.tensor_tensor(out=low[:], in0=pa[:], in1=pb[:], op=ALU.min)
         add_exps(PACK - 1)
-        nc.vector.tensor_tensor(out=hi[:], in0=pa[:], in1=pb[:], op=ALU.max)
-        for hf in range(2):
-            nc.scalar.activation(lse[:, :, half_cols(hf)], exsum[:, :, half_cols(hf)], ACT.Ln)
+        nc.vector.tensor_tensor(out=high[:], in0=pa[:], in1=pb[:], op=ALU.max)
+        for cols in HALVES:
+            nc.scalar.activation(log_sum[:, :, cols], ex_sum[:, :, cols], ACT.Ln)
         w3_dealt = sb.tile([P, N * PACK], BF16, name="w3_dealt", tag="w1q_codes", align_bytes=64)
         nc.scalar.activation(*dealt_views(w3_raw, w3_dealt, 0, P), ACT.Copy)
-        for hf in range(2):
-            nc.vector.tensor_tensor(out=above[:, :, half_cols(hf)], in0=yb[:, :, half_cols(hf)], in1=lo[:, :, half_cols(hf)], op=ALU.max)
-        for hf in range(2):
-            nc.vector.tensor_tensor(out=med[:, :, half_cols(hf)], in0=above[:, :, half_cols(hf)], in1=hi[:, :, half_cols(hf)], op=ALU.min)
-        z2_woven = [interleave(nc.vector.tensor_copy, med[:, :, half_cols(hf)], HALF, "z2_woven%d" % hf) for hf in range(2)]
+        for cols in HALVES:
+            nc.vector.tensor_tensor(out=above[:, :, cols], in0=own[:, :, cols], in1=low[:, :, cols], op=ALU.max)
+        for cols in HALVES:
+            nc.vector.tensor_tensor(out=z2[:, :, cols], in0=above[:, :, cols], in1=high[:, :, cols], op=ALU.min)
+        z2_woven = [weave(z2[:, :, cols], "z2_woven%d" % hf) for hf, cols in enumerate(HALVES)]
         z2q = [quantize(z2_woven[hf][:], HALF, "z2q%d" % hf) for hf in range(2)]
 
         diff = [sb.tile([P, PACK, HALF], F32, name="diff%d" % hf) for hf in range(2)]
-        zb = [sb.tile([P, PACK, HALF], BF16, name="zb%d" % hf) for hf in range(2)]
+        z = [sb.tile([P, PACK, HALF], BF16, name="z%d" % hf, tag="z%d" % hf, align_bytes=64) for hf in range(2)]
 
         def subtract(hf, t):
-            nc.vector.tensor_tensor(
-                out=diff[hf][:, t, :], in0=y[t][:].indirect(half_list(n2_l, hf)), in1=lse[:, t, half_cols(hf)], op=ALU.subtract
-            )
+            window = y_ex[t][:].indirect(entries(n2_l, HALVES[hf]))
+            nc.vector.tensor_tensor(out=diff[hf][:, t, :], in0=window, in1=log_sum[:, t, HALVES[hf]], op=ALU.subtract)
 
-        def gain(hf, t):
-            nc.vector.tensor_scalar(
-                out=zb[hf][:, t, :], in0=diff[hf][:, t, :], scalar1=gn_t[:, t : t + 1], scalar2=-1.0, op0=ALU.mult, op1=ALU.mult
-            )
+        def gain_on_vector(hf, t):
+            nc.vector.tensor_scalar(out=z[hf][:, t, :], in0=diff[hf][:, t, :], scalar1=neg_gn[:, t : t + 1], scalar2=None, op0=ALU.mult)
 
         for t in range(PACK):
             subtract(0, t)
-            nc.scalar.activation(zb[0][:, t, :], diff[0][:, t, :], ACT.Copy, scale=neg_gn[:, t : t + 1])
-        w2_dealt = sb.tile([P, N * PACK], BF16, name="w2_dealt", align_bytes=64)
+            nc.scalar.activation(z[0][:, t, :], diff[0][:, t, :], ACT.Copy, scale=neg_gn[:, t : t + 1])
+        w2_dealt = sb.tile([P, N * PACK], BF16, name="w2_dealt", tag="w1q_scales", align_bytes=64)
         nc.scalar.activation(*dealt_views(w2_raw, w2_dealt, 0, P), ACT.Copy)
-        warm = sb.tile([P, 1], F32, name="warm")
-        nc.scalar.activation(warm[:], lse[:, PACK - 1, S - 1 : S], ACT.Sigmoid)
         w3q = quantize(w3_dealt[:], N, "w3q")
         subtract(1, 0)
-        z_woven0 = interleave(nc.vector.tensor_copy, zb[0][:], HALF, "z_woven0")
+        z_woven0 = weave(z[0][:], "z_woven0")
         subtract(1, 1)
-        zq0 = quantize(z_woven0[:], HALF, "zq0")
+        zq = [quantize(z_woven0[:], HALF, "zq0")]
         w2q = quantize(w2_dealt[:], N, "w2q")
-        subtract(1, 2)
-        gain(1, 0)
-        subtract(1, 3)
-        gain(1, 1)
-        gain(1, 2)
-        gain(1, 3)
-        z_woven1 = interleave(nc.vector.tensor_copy, zb[1][:], HALF, "z_woven1")
-        zq1 = quantize(z_woven1[:], HALF, "zq1")
-        zq = [zq0, zq1]
+        for t in range(2, PACK):
+            subtract(1, t)
+            gain_on_vector(1, t - 2)
+        for t in range(PACK - 2, PACK):
+            gain_on_vector(1, t)
+        zq.append(quantize(weave(z[1][:], "z_woven1")[:], HALF, "zq1"))
 
-        h = [sb.tile([P, 2 * S], F32, name="h%d" % t) for t in range(PACK)]
-        sig = [sb.tile([P, 2 * S], F32, name="sig%d" % t) for t in range(PACK)]
-        for hf in range(2):
+        h_tags = ["h0", "h1", "z1", "z_woven1"]
+        h = [sb.tile([P, 2 * S], F32, name="h%d" % t, tag=h_tags[t], align_bytes=64) for t in range(PACK)]
+        gate = [sb.tile([P, 2 * S], F32, name="gate%d" % t) for t in range(PACK)]
+        res = [sb.tile([P, S], F32, name="res%d" % t) for t in range(PACK)]
+        for hf, cols in enumerate(HALVES):
             for t in range(PACK):
-                acc = ps.tile([P, HALF], F32, name="h_ps%d_%d" % (hf, t), tag="bank%d" % ((t + 1) % PACK + PACK if hf == 0 else t))
-                product(acc[:], w3q, t, z2q[hf], slice(0, HALF), True, False)
-                product(acc[:], w2q, t, zq[hf], slice(0, HALF), False, True)
-                if t < 2:
-                    nc.scalar.activation(sig[t][:, half_cols(hf)], acc[:], ACT.Sigmoid)
-                if t < 2 and hf == 1:
-                    nc.vector.tensor_copy(out=h[t][:, half_cols(hf)], in_=acc[:])
+                bank = PACK + (t + 1) % PACK if hf == 0 else t
+                acc = ps.tile([P, HALF], F32, name="h_ps%d_%d" % (hf, t), tag="bank%d" % bank)
+                product(acc, w3q, t, z2q[hf], slice(0, HALF), True, False)
+                product(acc, w2q, t, zq[hf], slice(0, HALF), False, True)
+                if t < FUSED_PLANES:
+                    nc.scalar.activation(gate[t][:, cols], acc[:], ACT.Sigmoid)
+                if hf == 0 and t >= FUSED_PLANES:
+                    nc.vector.tensor_copy(out=h[t][:, cols], in_=acc[:])
                 else:
-                    nc.scalar.activation(h[t][:, half_cols(hf)], acc[:], ACT.Copy)
+                    nc.scalar.activation(h[t][:, cols], acc[:], ACT.Copy)
 
         out_rows = out.rearrange("(p t) n -> t p n", t=PACK)
-        res = [sb.tile([P, S], F32, name="res%d" % t) for t in range(PACK)]
-        for t in range(2):
-            nc.vector.tensor_tensor(out=res[t][:], in0=sig[t][:].indirect(n5_l[:]), in1=h[t][:, :S], op=ALU.mult)
+        for t in range(FUSED_PLANES):
+            nc.vector.tensor_tensor(out=res[t][:], in0=gate[t][:].indirect(n5_l[:]), in1=h[t][:, :S], op=ALU.mult)
             nc.sync.dma_start(out_rows[t], res[t][:])
-        nc.scalar.activation(sig[2][:, :S], h[2][:].indirect(n5_l[:]), ACT.Sigmoid)
-        nc.vector.tensor_tensor(out=res[2][:], in0=sig[2][:, :S], in1=h[2][:, :S], op=ALU.mult)
-        nc.sync.dma_start(out_rows[2], res[2][:])
-        for hf in range(2):
-            cols = half_cols(hf)
-            nc.scalar.activation(sig[3][:, cols], h[3][:].indirect(half_list(n5_l, hf)), ACT.Sigmoid)
-            nc.vector.tensor_tensor(out=res[3][:, cols], in0=sig[3][:, cols], in1=h[3][:, cols], op=ALU.mult)
-            nc.sync.dma_start(out_rows[3][:, cols], res[3][:, cols])
+        for t in range(FUSED_PLANES, PACK):
+            for cols in HALVES if t == PACK - 1 else (slice(0, S),):
+                nc.scalar.activation(gate[t][:, cols], h[t][:].indirect(entries(n5_l, cols)), ACT.Sigmoid)
+                nc.vector.tensor_tensor(out=res[t][:, cols], in0=gate[t][:, cols], in1=h[t][:, cols], op=ALU.mult)
+                nc.sync.dma_start(out_rows[t][:, cols], res[t][:, cols])

@@ -137,7 +137,7 @@ def tile_picked_joinlsemedgate_none_p_kernel(
             nc.scalar.activation(dst, acc[:], ACT.Copy, scale=gm_t[:, t : t + 1])
 
         def add_exps(t):
-            nc.vector.tensor_tensor(out=ex_sum[:, t, :], in0=y_ex[t][:, S:], in1=ex_n1[:, t, :], op=ALU.add)
+            (nc.gpsimd if t < 2 else nc.vector).tensor_tensor(out=ex_sum[:, t, :], in0=y_ex[t][:, S:], in1=ex_n1[:, t, :], op=ALU.add)
 
         (first_cols, first_acc), (second_cols, second_acc) = y_ps[0]
         nc.vector.tensor_scalar(out=gm_y[0][:, first_cols], in0=first_acc[:], scalar1=gm_t[:, 0:1], scalar2=None, op0=ALU.mult)
@@ -152,7 +152,9 @@ def tile_picked_joinlsemedgate_none_p_kernel(
             nc.scalar.activation(ex_n1[:, t, :], y_ex[t][:].indirect(n1_l[:]), ACT.Exp)
             nc.vector.tensor_copy(out=pa[:, t, :], in_=gm_y[t][:].indirect(n3_l[:]))
             nc.vector.tensor_copy(out=pb[:, t, :], in_=gm_y[t][:].indirect(n4_l[:]))
-        for t in range(PACK):
+        for t in range(3):
+            nc.gpsimd.tensor_scalar(out=own[:, t, :], in0=gm_y[t][:, :S], scalar1=1.0, scalar2=0.0, op0=ALU.mult, op1=ALU.add)
+        for t in range(3, PACK):
             for cols, acc in y_ps[t]:
                 scale_y(own[:, t, cols], t, acc)
 

from contextlib import ExitStack

import concourse.mybir as mybir

K, T, S, H, N = 512, 2048, 512, 512, 512
FLOPS = 2 * K * H * S + 2 * 2 * H * N * S

F32 = mybir.dt.float32
BF16 = mybir.dt.bfloat16
I32 = mybir.dt.int32
U32 = mybir.dt.uint32
U16 = mybir.dt.uint16
U8 = mybir.dt.uint8
FP8X4 = mybir.dt.float8_e4m3fn_x4
ACT = mybir.ActivationFunctionType
ALU = mybir.AluOpType

P = 128
PACK = 4
HALF = S // 2
HALVES = (slice(0, HALF), slice(HALF, S))
W1_SCALAR_COLS = 64
FUSED_PLANES = 2


def tile_picked_joinlsemedgate_none_p_kernel(
    tc, x_words, x_scales, w1, gn, gm, w2, w3, offs, n1, n2, n3, n4, n5, out
):
    nc = tc.nc
    with ExitStack() as ctx:
        sb = ctx.enter_context(tc.tile_pool(name="sb", bufs=1))
        ps = ctx.enter_context(tc.psum_pool(name="ps", bufs=1))

        def load_list(src, name):
            lst = sb.tile([P, S // 16], U16, name=name)
            nc.sync.dma_start(lst[:], src)
            return lst

        def load_weight(src, name):
            raw = sb.tile([P, PACK, H], F32, name=name)
            nc.sync.dma_start(raw[:], src.rearrange("(p j) c -> p j c", j=PACK))
            return raw

        def load_gain(src, name):
            gain = sb.tile([P, PACK], F32, name=name)
            nc.sync.dma_start(gain[:], src.rearrange("(p t) o -> p (t o)", t=PACK))
            return gain

        def entries(lst, cols):
            return lst[:, cols.start // 16 : cols.stop // 16]

        def dealt_views(raw, dealt, m0, m1):
            src = raw[:].rearrange("p j (m t) -> p m t j", t=PACK)[:, m0:m1]
            dst = dealt[:].rearrange("p (t m j) -> p m t j", t=PACK, j=PACK)[:, m0:m1]
            return dst, src

        def quantize(values, width, name):
            codes = sb.tile([P, width], U32, name=name + "_codes", tag=name + "_codes", align_bytes=64)
            scales = sb.tile([P, width], U8, name=name + "_scales", tag=name + "_scales", align_bytes=64)
            nc.vector.quantize_mx(out=codes[:].bitcast(FP8X4), scales=scales[:], in_=values)
            return codes, scales

        def weave(planes, name):
            woven = sb.tile([P, HALF * PACK], BF16, name=name, tag=name, align_bytes=64)
            nc.vector.tensor_copy(
                out=woven[:].rearrange("p (c i t) -> p c t i", i=PACK, t=PACK),
                in_=planes.rearrange("p t (c i) -> p c t i", i=PACK),
            )
            return woven

        def product(acc, wq, t, xq, cols, start, stop):
            m_cols = slice(t * P, (t + 1) * P)
            nc.tensor.matmul_mx(
                out=acc[:],
                lhsT=wq[0][:, m_cols].bitcast(FP8X4),
                lhsT_scale=wq[1][:, m_cols],
                rhs=xq[0][:, cols].bitcast(FP8X4),
                rhs_scale=xq[1][:, cols],
                start=start,
                stop=stop,
            )

        scale_table = sb.tile([P, T], U8, name="scale_table")
        nc.vector.memset(scale_table[:].bitcast(I32), 0)
        offs_l = load_list(offs, "offs_l")
        w1_raw = load_weight(w1, "w1_raw")
        for r in range(PACK):
            nc.sync.dma_start(scale_table[r:P:32, :].bitcast(I32), x_scales[0, r:16:PACK, :].bitcast(I32))
        word_table = sb.tile([P, T], U32, name="word_table")
        nc.sync.dma_start(word_table[:].bitcast(I32), x_words[0].rearrange("p c r -> p (c r)").bitcast(I32))
        gm_t = load_gain(gm, "gm_t")
        n3_l = load_list(n3, "n3_l")
        n4_l = load_list(n4, "n4_l")
        n1_l = load_list(n1, "n1_l")
        gn_t = load_gain(gn, "gn_t")
        n2_l = load_list(n2, "n2_l")
        n5_l = load_list(n5, "n5_l")
        w3_raw = load_weight(w3, "w3_raw")
        w2_raw = load_weight(w2, "w2_raw")

        w1_dealt = sb.tile([P, H * PACK], BF16, name="w1_dealt", align_bytes=64)
        nc.scalar.activation(*dealt_views(w1_raw, w1_dealt, 0, W1_SCALAR_COLS), ACT.Copy)
        nc.vector.tensor_copy(*dealt_views(w1_raw, w1_dealt, W1_SCALAR_COLS, P))
        x_picked_scales = sb.tile([P, S], U8, name="x_picked_scales", align_bytes=64)
        nc.vector.tensor_copy(out=x_picked_scales[:], in_=scale_table[:].indirect(offs_l[:]))
        w1q = quantize(w1_dealt[:], H, "w1q")
        x_picked_words = sb.tile([P, S], U32, name="x_picked_words", align_bytes=64)
        for cols in HALVES:
            nc.vector.tensor_copy(out=x_picked_words[:, cols], in_=word_table[:].indirect(entries(offs_l, cols)))
        xq = (x_picked_words, x_picked_scales)
        neg_gn = sb.tile([P, PACK], F32, name="neg_gn")
        nc.scalar.activation(neg_gn[:], gn_t[:], ACT.Copy, scale=-1.0)

        y_ps = []
        for t in range(PACK):
            pieces = []
            for k, cols in enumerate(HALVES if t == 0 else (slice(0, S),)):
                acc = ps.tile([P, cols.stop - cols.start], F32, name="y_ps%d_%d" % (t, k), tag="bank%d" % (t + PACK * k))
                product(acc, w1q, t, xq, cols, True, True)
                pieces.append((cols, acc))
            y_ps.append(pieces)

        gm_y = [sb.tile([P, 2 * S], F32, name="gm_y%d" % t) for t in range(PACK)]
        y_ex = [sb.tile([P, 2 * S], F32, name="y_ex%d" % t) for t in range(PACK)]
        ex_n1 = sb.tile([P, PACK, S], F32, name="ex_n1")
        ex_sum = sb.tile([P, PACK, S], F32, name="ex_sum")
        log_sum = sb.tile([P, PACK, S], F32, name="log_sum")
        own = sb.tile([P, PACK, S], BF16, name="own")
        pa = sb.tile([P, PACK, S], BF16, name="pa")
        pb = sb.tile([P, PACK, S], BF16, name="pb")
        low = sb.tile([P, PACK, S], BF16, name="low")
        high = sb.tile([P, PACK, S], BF16, name="high")
        above = sb.tile([P, PACK, S], BF16, name="above")
        z2 = sb.tile([P, PACK, S], BF16, name="z2")

        def scale_y(dst, t, acc):
            nc.scalar.activation(dst, acc[:], ACT.Copy, scale=gm_t[:, t : t + 1])

        def add_exps(t):
            (nc.gpsimd if t < 2 else nc.vector).tensor_tensor(out=ex_sum[:, t, :], in0=y_ex[t][:, S:], in1=ex_n1[:, t, :], op=ALU.add)

        (first_cols, first_acc), (second_cols, second_acc) = y_ps[0]
        nc.vector.tensor_scalar(out=gm_y[0][:, first_cols], in0=first_acc[:], scalar1=gm_t[:, 0:1], scalar2=None, op0=ALU.mult)
        scale_y(gm_y[0][:, second_cols], 0, second_acc)
        for t in range(PACK):
            if t + 1 < PACK:
                for cols, acc in y_ps[t + 1]:
                    scale_y(gm_y[t + 1][:, cols], t + 1, acc)
            for cols, acc in y_ps[t]:
                nc.scalar.activation(y_ex[t][:, cols], acc[:], ACT.Copy)
                nc.scalar.activation(y_ex[t][:, S + cols.start : S + cols.stop], acc[:], ACT.Exp)
            nc.scalar.activation(ex_n1[:, t, :], y_ex[t][:].indirect(n1_l[:]), ACT.Exp)
            nc.vector.tensor_copy(out=pa[:, t, :], in_=gm_y[t][:].indirect(n3_l[:]))
            nc.vector.tensor_copy(out=pb[:, t, :], in_=gm_y[t][:].indirect(n4_l[:]))
        for t in range(3):
            nc.gpsimd.tensor_scalar(out=own[:, t, :], in0=gm_y[t][:, :S], scalar1=1.0, scalar2=0.0, op0=ALU.mult, op1=ALU.add)
        for t in range(3, PACK):
            for cols, acc in y_ps[t]:
                scale_y(own[:, t, cols], t, acc)

        for t in range(PACK - 1):
            add_exps(t)
        nc.vector.tensor_tensor(out=low[:], in0=pa[:], in1=pb[:], op=ALU.min)
        add_exps(PACK - 1)
        nc.vector.tensor_tensor(out=high[:], in0=pa[:], in1=pb[:], op=ALU.max)
        for cols in HALVES:
            nc.scalar.activation(log_sum[:, :, cols], ex_sum[:, :, cols], ACT.Ln)
        w3_dealt = sb.tile([P, N * PACK], BF16, name="w3_dealt", tag="w1q_codes", align_bytes=64)
        nc.scalar.activation(*dealt_views(w3_raw, w3_dealt, 0, P), ACT.Copy)
        for cols in HALVES:
            nc.vector.tensor_tensor(out=above[:, :, cols], in0=own[:, :, cols], in1=low[:, :, cols], op=ALU.max)
        for cols in HALVES:
            nc.vector.tensor_tensor(out=z2[:, :, cols], in0=above[:, :, cols], in1=high[:, :, cols], op=ALU.min)
        z2_woven = [weave(z2[:, :, cols], "z2_woven%d" % hf) for hf, cols in enumerate(HALVES)]
        z2q = [quantize(z2_woven[hf][:], HALF, "z2q%d" % hf) for hf in range(2)]

        diff = [sb.tile([P, PACK, HALF], F32, name="diff%d" % hf) for hf in range(2)]
        z = [sb.tile([P, PACK, HALF], BF16, name="z%d" % hf, tag="z%d" % hf, align_bytes=64) for hf in range(2)]

        def subtract(hf, t):
            window = y_ex[t][:].indirect(entries(n2_l, HALVES[hf]))
            nc.vector.tensor_tensor(out=diff[hf][:, t, :], in0=window, in1=log_sum[:, t, HALVES[hf]], op=ALU.subtract)

        def gain_on_vector(hf, t):
            nc.vector.tensor_scalar(out=z[hf][:, t, :], in0=diff[hf][:, t, :], scalar1=neg_gn[:, t : t + 1], scalar2=None, op0=ALU.mult)

        for t in range(PACK):
            subtract(0, t)
            nc.scalar.activation(z[0][:, t, :], diff[0][:, t, :], ACT.Copy, scale=neg_gn[:, t : t + 1])
        w2_dealt = sb.tile([P, N * PACK], BF16, name="w2_dealt", tag="w1q_scales", align_bytes=64)
        nc.scalar.activation(*dealt_views(w2_raw, w2_dealt, 0, P), ACT.Copy)
        w3q = quantize(w3_dealt[:], N, "w3q")
        subtract(1, 0)
        z_woven0 = weave(z[0][:], "z_woven0")
        subtract(1, 1)
        zq = [quantize(z_woven0[:], HALF, "zq0")]
        w2q = quantize(w2_dealt[:], N, "w2q")
        for t in range(2, PACK):
            subtract(1, t)
            gain_on_vector(1, t - 2)
        for t in range(PACK - 2, PACK):
            gain_on_vector(1, t)
        zq.append(quantize(weave(z[1][:], "z_woven1")[:], HALF, "zq1"))

        h_tags = ["h0", "h1", "z1", "z_woven1"]
        h = [sb.tile([P, 2 * S], F32, name="h%d" % t, tag=h_tags[t], align_bytes=64) for t in range(PACK)]
        gate = [sb.tile([P, 2 * S], F32, name="gate%d" % t) for t in range(PACK)]
        res = [sb.tile([P, S], F32, name="res%d" % t) for t in range(PACK)]
        for hf, cols in enumerate(HALVES):
            for t in range(PACK):
                bank = PACK + (t + 1) % PACK if hf == 0 else t
                acc = ps.tile([P, HALF], F32, name="h_ps%d_%d" % (hf, t), tag="bank%d" % bank)
                product(acc, w3q, t, z2q[hf], slice(0, HALF), True, False)
                product(acc, w2q, t, zq[hf], slice(0, HALF), False, True)
                if t < FUSED_PLANES:
                    nc.scalar.activation(gate[t][:, cols], acc[:], ACT.Sigmoid)
                if hf == 0 and t >= FUSED_PLANES:
                    nc.vector.tensor_copy(out=h[t][:, cols], in_=acc[:])
                else:
                    nc.scalar.activation(h[t][:, cols], acc[:], ACT.Copy)

        out_rows = out.rearrange("(p t) n -> t p n", t=PACK)
        for t in range(FUSED_PLANES):
            nc.vector.tensor_tensor(out=res[t][:], in0=gate[t][:].indirect(n5_l[:]), in1=h[t][:, :S], op=ALU.mult)
            nc.sync.dma_start(out_rows[t], res[t][:])
        for t in range(FUSED_PLANES, PACK):
            for cols in HALVES if t == PACK - 1 else (slice(0, S),):
                nc.scalar.activation(gate[t][:, cols], h[t][:].indirect(entries(n5_l, cols)), ACT.Sigmoid)
                nc.vector.tensor_tensor(out=res[t][:, cols], in0=gate[t][:, cols], in1=h[t][:, cols], op=ALU.mult)
                nc.sync.dma_start(out_rows[t][:, cols], res[t][:, cols])
